import numpy as np
import ml_dtypes


def mxq(x, axis, fmt="e4m3"):
    dtype, down = {"e4m3": (ml_dtypes.float8_e4m3fn, 7), "e5m2": (ml_dtypes.float8_e5m2, 14)}[fmt]
    v = np.moveaxis(np.asarray(x, np.float32).astype(ml_dtypes.bfloat16).astype(np.float64), axis, -1)
    blocks = v.reshape(v.shape[:-1] + (-1, 32))
    amax = np.abs(blocks).max(-1, keepdims=True)
    byte = np.maximum(np.where(amax > 0, np.frexp(amax)[1] - 1 + 127, 0) - down, 1)
    scale = np.exp2(byte - 127.0)
    codes = (blocks / scale).astype(np.float32).astype(dtype).astype(np.float64)
    return np.moveaxis((codes * scale).reshape(v.shape), -1, axis)


WIDE = False


def mx_kscale(k):
    if not WIDE:
        return np.ones(k)
    levels = np.array([10, -10, 5, -5, 0])
    if k % 512:
        return np.exp2(np.random.permutation(np.resize(levels, k // 32))).repeat(32)
    a = np.empty((k // 512, 16))
    for p in range(k // 512):
        a[p, :8] = np.random.permutation(np.resize(levels, 8))
        for g in range(8):
            far = levels[np.abs(levels - a[p, g]) >= 10]
            a[p, g + 8] = far[np.random.randint(len(far))]
    return np.exp2(a.ravel()).repeat(32)


def f64(x):
    return np.asarray(x).astype(np.float64)


def striped(idx):
    return np.tile(idx.reshape(-1, 16).T, (8, 1)).astype(np.uint16)


def unstriped(offs):
    return offs[:16].T.reshape(-1).astype(np.int64)


E2M1 = np.array([0.0, 0.5, 1.0, 1.5, 2.0, 3.0, 4.0, 6.0, -0.0, -0.5, -1.0, -1.5, -2.0, -3.0, -4.0, -6.0])


def pack_weight(w, fmt):
    k, n = w.shape
    w = f64(np.asarray(w, np.float32).astype(ml_dtypes.bfloat16)).reshape(k // 32, 32, n)
    amax = np.abs(w).max(1)
    if fmt == "e4m3":
        byte = np.frexp(amax)[1] - 1 + 127 - 7
    else:
        mant, ex = np.frexp(amax / 6.0)
        byte = np.where(mant > 0.5, ex, ex - 1) + 127
    byte = np.clip(np.where(amax > 0, byte, 1), 1, 254)
    scaled = (w * np.exp2(127.0 - byte)[:, None, :]).reshape(k, n).astype(np.float32)
    by_word = np.ascontiguousarray(scaled.reshape(k // 512, 128, 4, n).transpose(0, 1, 3, 2))
    if fmt == "e4m3":
        words = by_word.astype(ml_dtypes.float8_e4m3fn).view(np.uint8)
    else:
        c = by_word.astype(ml_dtypes.float4_e2m1fn).view(np.uint8) & 0xF
        words = (c[..., 0::2] | (c[..., 1::2] << 4)).reshape(k // 512, 128, 2 * n)
    return np.ascontiguousarray(words), np.ascontiguousarray(byte.astype(np.uint8).reshape(k // 512, 16, n))


def unpack_weight(words, scales, fmt):
    g, _, n = scales.shape
    words = np.ascontiguousarray(words).reshape(g, 128, n, -1)
    if fmt == "e4m3":
        vals = words.view(ml_dtypes.float8_e4m3fn).astype(np.float64)
    else:
        nib = np.empty((g, 128, n, 4), np.uint8)
        nib[..., 0::2] = words & 0xF
        nib[..., 1::2] = words >> 4
        vals = E2M1[nib]
    vals = vals * np.repeat(np.exp2(scales.astype(np.float64) - 127.0), 8, axis=1)[..., None]
    return vals.transpose(0, 1, 3, 2).reshape(g * 512, n)


def gelu(v):
    return 0.5 * v * (1.0 + np.tanh(np.sqrt(2.0 / np.pi) * (v + 0.044715 * v**3)))


K, H, T, S, T2, T3, S2, P = 1024, 1024, 2048, 512, 1024, 2048, 512, 512

def setup_inputs():
    n = np.random.standard_normal
    s = mx_kscale(K)[:, None]
    u = mx_kscale(H)[:, None]
    tab_words, tab_scales = pack_weight(n((K, T)) * s, "e4m3")
    tab2_words, tab2_scales = pack_weight(n((H, T3)) / np.sqrt(H) / u, "e4m3")
    w4_words, w4_scales = pack_weight(n((K, H)) / np.sqrt(K) / s * u.T, "e2m1")
    return {
        "tab_words": tab_words, "tab_scales": tab_scales,
        "tab2_words": tab2_words, "tab2_scales": tab2_scales,
        "w1": (n((K, H)) / np.sqrt(K) / s * u.T).astype(np.float32),
        "w4_words": w4_words, "w4_scales": w4_scales,
        "page0": (n((H, T2)) * u).astype(np.float32),
        "wgs": np.exp(0.3 * n((128, S))).astype(np.float32),
        "gain": np.exp(0.3 * n(H)).astype(np.float32),
        "seam": n(S2).astype(np.float32),
        "offs": striped(np.random.permutation(T)[:S]),
        "offs2": striped(np.random.permutation(T3)[:S2]),
        "offs3": striped(np.random.permutation(T2)[:S]),
        "pos1": striped(np.random.permutation(T2)[:P]),
        "pos2": striped(np.random.permutation(T2)[:P]),
    }

def reference(tab_words, tab_scales, tab2_words, tab2_scales, w1, w4_words, w4_scales,
              page0, wgs, gain, seam, offs, offs2, offs3, pos1, pos2):
    v = unpack_weight(tab_words, tab_scales, "e4m3")[:, unstriped(offs)]
    v2 = unpack_weight(tab2_words, tab2_scales, "e4m3")[:, unstriped(offs2)]
    w1q = mxq(f64(w1), 0, "e4m3")
    w4 = unpack_weight(w4_words, w4_scales, "e2m1")
    h = np.maximum(w1q.T @ v, w4.T @ v)
    page = f64(page0).copy()
    page[:, unstriped(offs3)] = np.tile(f64(wgs), (H // 128, 1)) * h
    x = mxq(f64(gain)[:, None] * page, 0, "e4m3")
    e = v2.T @ x
    d = np.abs(e[:, unstriped(pos1)] - e[:, unstriped(pos2)])
    return d + f64(seam)[:, None]

@@ -1,0 +1,285 @@
+from contextlib import ExitStack
+
+import concourse.mybir as mybir
+
+K, H, T, S, T2, T3, S2, PAIRS = 1024, 1024, 2048, 512, 1024, 2048, 512, 512
+FLOPS = 2 * K * H * S * 2 + 2 * H * S2 * T2
+
+F32 = mybir.dt.float32
+BF16 = mybir.dt.bfloat16
+I32 = mybir.dt.int32
+U32 = mybir.dt.uint32
+U16 = mybir.dt.uint16
+U8 = mybir.dt.uint8
+FP8X4 = mybir.dt.float8_e4m3fn_x4
+FP4X4 = mybir.dt.float4_e2m1fn_x4
+ALU = mybir.AluOpType
+ACT = mybir.ActivationFunctionType
+
+P = 128
+PACK = 4
+PASS = P * PACK
+BANK = 512
+W1_VECTOR_SHARE = 88
+
+
+def tile_list_shearer_horizon_scores_kernel(
+    tc, tab_words, tab_scales, tab2_words, tab2_scales, w1, w4_words, w4_scales,
+    page0, wgs, gain, seam, offs, offs2, offs3, pos1, pos2, out,
+):
+    nc = tc.nc
+    with ExitStack() as ctx:
+        sb = ctx.enter_context(tc.tile_pool(name="sb", bufs=1))
+        ps = ctx.enter_context(tc.psum_pool(name="ps", bufs=1))
+
+        def new(shape, dtype, name, tag=None, bufs=1):
+            return sb.tile(shape, dtype, name=name, tag=tag or name, bufs=bufs, align_bytes=64)
+
+        def load_list(src, name):
+            t = new([P, 32], U16, name)
+            nc.sync.dma_start(t[:], src)
+            return t
+
+        def load_words(src, a, name):
+            t = new([P, T], I32, name)
+            nc.sync.dma_start(t[:], src[a].rearrange("p t i -> p (t i)").bitcast(I32))
+            return t
+
+        def load_w1(a, b):
+            t = new([P, PACK, PASS], F32, f"w1raw{a}{b}")
+            nc.sync.dma_start(
+                t[:], w1[a * PASS : (a + 1) * PASS, b * PASS : (b + 1) * PASS].rearrange("(p j) c -> p j c", j=PACK)
+            )
+            return t
+
+        def load_w4(b):
+            t = new([P, 2, 2 * PASS], U8, f"w4_raw{b}")
+            nc.sync.dma_start(
+                t[:].bitcast(I32),
+                w4_words[:, :, 2 * PASS * b : 2 * PASS * (b + 1)].bitcast(I32).rearrange("a p c -> p a c"),
+            )
+            return t
+
+        def load_page(b, t):
+            pg = new([P, T2], F32, f"page{b}{t}")
+            nc.sync.dma_start(pg[:], page0[b * PASS : (b + 1) * PASS, :].rearrange("(p t) n -> p t n", t=PACK)[:, t, :])
+            return pg
+
+        def load_wgs(t0, t1, name):
+            w = new([P, t1 - t0, S], F32, name)
+            for q in range(4):
+                nc.sync.dma_start(w[32 * q : 32 * (q + 1)], wgs.rearrange("(p t) j -> p t j", t=PACK)[:, t0:t1, :])
+            return w
+
+        tab_sc = new([P, 2, T], U8, "tab_sc")
+        nc.vector.memset(tab_sc[:].rearrange("p a t -> p (a t)").bitcast(I32), 0)
+        w4_sc = new([P, 2, H], U8, "w4_sc")
+        nc.gpsimd.memset(w4_sc[:].rearrange("p a t -> p (a t)").bitcast(I32), 0)
+        tab2_sc = new([P, T3], U8, "tab2_sc")
+        nc.gpsimd.memset(tab2_sc[:].bitcast(I32), 0)
+
+        tab_w = [load_words(tab_words, 0, "tab_w0")]
+        idx = load_list(offs, "idx")
+        for r in range(4):
+            nc.sync.dma_start(
+                tab_sc[r:P:32].bitcast(I32), tab_scales.bitcast(I32).rearrange("a (q r) t -> r q a t", r=4)[r]
+            )
+        tab_w.append(load_words(tab_words, 1, "tab_w1"))
+        w4_raw = [load_w4(0)]
+        for r in range(4):
+            nc.sync.dma_start(
+                w4_sc[r:P:32].bitcast(I32), w4_scales.bitcast(I32).rearrange("a (q r) t -> r q a t", r=4)[r]
+            )
+        w1_raw = {(0, 0): load_w1(0, 0), (1, 0): load_w1(1, 0)}
+        idx3 = load_list(offs3, "idx3")
+        pages = {(0, 0): load_page(0, 0)}
+        wgs_first = load_wgs(0, 1, "wgs_first")
+        pages[0, 1] = load_page(0, 1)
+        wgs_rest = load_wgs(1, 4, "wgs_rest")
+        w4_raw.append(load_w4(1))
+        w1_raw[0, 1] = load_w1(0, 1)
+        w1_raw[1, 1] = load_w1(1, 1)
+        pages[0, 2] = load_page(0, 2)
+        gains = new([P, 2, PACK], F32, "gains")
+        nc.sync.dma_start(gains[:], gain.rearrange("(b p t) -> p b t", b=2, t=PACK))
+        pages[0, 3] = load_page(0, 3)
+        idx2 = load_list(offs2, "idx2")
+        pages[1, 0] = load_page(1, 0)
+        pages[1, 1] = load_page(1, 1)
+        for q in range(4):
+            nc.sync.dma_start(
+                tab2_sc[32 * q : 32 * q + 8, :].bitcast(I32), tab2_scales.bitcast(I32)[:, 4 * q : 4 * q + 4, :]
+            )
+        tab2_w = [load_words(tab2_words, a, f"tab2_w{a}") for a in range(2)]
+        pages[1, 2] = load_page(1, 2)
+        pages[1, 3] = load_page(1, 3)
+        p1 = load_list(pos1, "p1")
+        p2 = load_list(pos2, "p2")
+        seams = new([P, S2 // P], F32, "seams")
+        with nc.allow_non_contiguous_dma(reason="one offset for each candidate, on its partition"):
+            nc.sync.dma_start(seams[:], seam.rearrange("(m p) -> p m", p=P))
+
+        def wgs_of(t):
+            return wgs_first[:, 0, :] if t == 0 else wgs_rest[:, t - 1, :]
+
+        v_w, v_s = [], []
+        for a in range(2):
+            vw = new([P, S], U32, f"v_w{a}")
+            nc.vector.tensor_copy(vw[:], tab_w[a][:].bitcast(U32).indirect(idx[:]))
+            vs = new([P, S], U8, f"v_s{a}")
+            nc.vector.tensor_copy(vs[:], tab_sc[:, a, :].indirect(idx[:]))
+            v_w.append(vw)
+            v_s.append(vs)
+
+        w4_w, w4_s = [], []
+        for b in range(2):
+            ww = new([P, 2, 2 * PASS], U8, f"w4_w{b}")
+            nc.scalar.copy(
+                ww[:].bitcast(U16).rearrange("p a (t m) -> p a m t", t=PACK),
+                w4_raw[b][:].bitcast(U16).rearrange("p a (m t) -> p a m t", t=PACK),
+            )
+            ws = new([P, 2, PASS], U8, f"w4_s{b}")
+            nc.vector.tensor_copy(
+                ws[:].rearrange("p a (t m) -> p a m t", t=PACK),
+                w4_sc[:, :, b * PASS : (b + 1) * PASS].rearrange("p a (m t) -> p a m t", t=PACK),
+            )
+            w4_w.append(ww)
+            w4_s.append(ws)
+
+        def quantise_w1(a, b, vector_share):
+            grouped = new([P, PACK * PASS], BF16, f"w1_bf{a}{b}")
+            dst = grouped[:].rearrange("p (t m j) -> p m j t", t=PACK, j=PACK)
+            src = w1_raw[a, b][:].rearrange("p j (m t) -> p m j t", t=PACK)
+            if vector_share:
+                nc.vector.tensor_copy(dst[:, :vector_share], src[:, :vector_share])
+            nc.scalar.copy(dst[:, vector_share:], src[:, vector_share:])
+            codes = new([P, PASS], U32, f"w1_w{a}{b}")
+            scales = new([P, PASS], U8, f"w1_s{a}{b}")
+            cuts = (0, P, PASS) if (a, b) == (1, 0) else (0, PASS)
+            for c0, c1 in zip(cuts, cuts[1:]):
+                nc.vector.quantize_mx(
+                    codes[:, c0:c1].bitcast(FP8X4), scales[:, c0:c1], grouped[:, PACK * c0 : PACK * c1]
+                )
+            return codes, scales
+
+        def product_w4(b, t):
+            acc = ps.tile([P, BANK], F32, name=f"acc4_{b}{t}", tag=f"bank{2 + t % 2}")
+            for a in range(2):
+                nc.tensor.matmul_mx(
+                    acc[:],
+                    lhsT=w4_w[b][:, a, 2 * P * t : 2 * P * (t + 1)].bitcast(FP4X4),
+                    lhsT_scale=w4_s[b][:, a, P * t : P * (t + 1)],
+                    rhs=v_w[a][:].bitcast(FP8X4), rhs_scale=v_s[a][:],
+                    start=(a == 0), stop=(a == 1),
+                )
+            held = new([P, S], F32, f"sum4_{b}{t}")
+            nc.scalar.copy(held[:], acc[:])
+            return held
+
+        def refresh(b, t, w1q, h_tag=None):
+            sum4 = sums4[b, t]
+            acc = ps.tile([P, BANK], F32, name=f"acc1_{b}{t}", tag=f"bank{4 + t}")
+            for a in range(2):
+                nc.tensor.matmul_mx(
+                    acc[:],
+                    lhsT=w1q[a][0][:, P * t : P * (t + 1)].bitcast(FP8X4),
+                    lhsT_scale=w1q[a][1][:, P * t : P * (t + 1)],
+                    rhs=v_w[a][:].bitcast(FP8X4), rhs_scale=v_s[a][:],
+                    start=(a == 0), stop=(a == 1),
+                )
+            h = new([P, S], F32, f"h{b}{t}", tag=h_tag or "h", bufs=1 if h_tag else 2)
+            nc.vector.tensor_tensor(h[:], acc[:], sum4[:], ALU.max)
+            nc.vector.tensor_tensor(pages[b, t][:].indirect(idx3[:]), h[:], wgs_of(t), ALU.mult)
+
+        def quantise_x(b, half, grouped, codes, scales):
+            nc.vector.quantize_mx(
+                codes[:, half * BANK : (half + 1) * BANK].bitcast(FP8X4),
+                scales[:, half * BANK : (half + 1) * BANK],
+                grouped[:, half * BANK : (half + 1) * BANK, :].rearrange("p n t -> p (n t)"),
+            )
+
+        w1q0 = [quantise_w1(a, 0, W1_VECTOR_SHARE) for a in range(2)]
+        sums4 = {(0, 0): product_w4(0, 0)}
+        refresh(0, 0, w1q0)
+        sums4[0, 1] = product_w4(0, 1)
+        refresh(0, 1, w1q0)
+        for b, t in ((0, 2), (0, 3), (1, 0), (1, 1), (1, 2), (1, 3)):
+            sums4[b, t] = product_w4(b, t)
+        w1q1 = [quantise_w1(a, 1, 0) for a in range(2)]
+        refresh(0, 2, w1q0)
+        refresh(0, 3, w1q0, h_tag="w1_bf11")
+
+        planes = new([P, PACK, T2], BF16, "x_planes", tag="w1raw11")
+        for t in range(PACK):
+            nc.scalar.activation(planes[:, t, :], pages[0, t][:], ACT.Copy, scale=gains[:, 0, t : t + 1])
+        x_bf0 = new([P, T2, PACK], BF16, "x_bf0")
+        x_w = [new([P, T2], U32, f"x_w{b}") for b in range(2)]
+        x_s = [new([P, T2], U8, f"x_s{b}") for b in range(2)]
+        for half in range(2):
+            cols = slice(half * BANK, (half + 1) * BANK)
+            nc.scalar.copy(
+                x_bf0[:, cols, :].rearrange("p (c i) t -> p c t i", i=4),
+                planes[:, :, cols].rearrange("p t (c i) -> p c t i", i=4),
+            )
+
+        refresh(1, 0, w1q1)
+        refresh(1, 1, w1q1)
+
+        def gather_candidates(part, words_tag, scales_tag):
+            lst = idx2[:, 16 * part : 16 * (part + 1)]
+            words = new([P, 2, S2 // 2], U32, f"v2_w{part}", tag=words_tag)
+            for a in range(2):
+                nc.vector.tensor_copy(words[:, a, :], tab2_w[a][:].bitcast(U32).indirect(lst))
+            scales = new([P, S2 // 2], U8, f"v2_s{part}", tag=scales_tag)
+            nc.vector.tensor_copy(scales[:], tab2_sc[:].indirect(lst))
+            return words, scales
+
+        v2 = [gather_candidates(0, None, None)]
+        for half in range(2):
+            quantise_x(0, half, x_bf0, x_w[0], x_s[0])
+
+        x_bf1 = new([P, T2, PACK], BF16, "x_bf1", tag="w1raw11")
+        for t in range(2):
+            nc.scalar.activation(x_bf1[:, :, t], pages[1, t][:], ACT.Copy, scale=gains[:, 1, t : t + 1])
+        refresh(1, 2, w1q1, h_tag="x_bf0")
+        gain_now = new([P, 1], F32, "gain_now")
+        nc.scalar.copy(gain_now[:], gains[:, 1, 2:3])
+        nc.scalar.activation(x_bf1[:, :BANK, 2], pages[1, 2][:, :BANK], ACT.Copy, scale=gain_now[:])
+        nc.scalar.copy(gain_now[:], gains[:, 1, 3:4])
+        nc.scalar.activation(x_bf1[:, BANK:, 2], pages[1, 2][:, BANK:], ACT.Copy, scale=gains[:, 1, 2:3])
+        refresh(1, 3, w1q1)
+        nc.vector.tensor_scalar(x_bf1[:, :BANK, 3], pages[1, 3][:, :BANK], gain_now[:], None, ALU.mult)
+        nc.scalar.activation(x_bf1[:, BANK:, 3], pages[1, 3][:, BANK:], ACT.Copy, scale=gains[:, 1, 3:4])
+        for half in range(2):
+            quantise_x(1, half, x_bf1, x_w[1], x_s[1])
+        v2.append(gather_candidates(1, "gain_now", "page13"))
+
+        for m in range(S2 // P):
+            rows = slice(m * P, (m + 1) * P)
+            e = new([P, T2], F32, f"e{m}", tag=f"page0{m}")
+            v2_w, v2_s = v2[m // 2]
+            cand = slice((m % 2) * P, (m % 2 + 1) * P)
+            for half in range(2):
+                cols = slice(half * BANK, (half + 1) * BANK)
+                acc = ps.tile([P, BANK], F32, name=f"acc_e{m}{half}", tag=f"bank{2 * m + half}")
+                for b in range(2):
+                    nc.tensor.matmul_mx(
+                        acc[:],
+                        lhsT=v2_w[:, b, cand].bitcast(FP8X4), lhsT_scale=v2_s[4 * b :, cand],
+                        rhs=x_w[b][:, cols].bitcast(FP8X4), rhs_scale=x_s[b][:, cols],
+                        start=(b == 0), stop=(b == 1),
+                    )
+                nc.scalar.copy(e[:, cols], acc[:])
+            pieces = 2
+            width = PAIRS // pieces
+            for piece in range(pieces):
+                lst = slice(piece * width // 16, (piece + 1) * width // 16)
+                floor = new([P, width], F32, f"floor{m}{piece}", tag="floor", bufs=4)
+                nc.vector.tensor_copy(floor[:], e[:].indirect(p2[:, lst]))
+                diff = new([P, width], F32, f"diff{m}{piece}", tag="diff", bufs=4)
+                nc.vector.tensor_tensor(diff[:], e[:].indirect(p1[:, lst]), floor[:], ALU.subtract)
+                size = new([P, width], F32, f"size{m}{piece}", tag="size", bufs=4)
+                nc.scalar.activation(size[:], diff[:], ACT.Abs)
+                res = new([P, width], F32, f"res{m}{piece}", tag="res", bufs=4)
+                nc.scalar.activation(res[:], size[:], ACT.Identity, bias=seams[:, m : m + 1])
+                nc.sync.dma_start(out[rows, piece * width : (piece + 1) * width], res[:])

@@ -20,7 +20,6 @@ P = 128
 PACK = 4
 PASS = P * PACK
 BANK = 512
-W1_VECTOR_SHARE = 88
 
 
 def tile_list_shearer_horizon_scores_kernel(
@@ -65,10 +64,10 @@ def tile_list_shearer_horizon_scores_kernel(
             nc.sync.dma_start(pg[:], page0[b * PASS : (b + 1) * PASS, :].rearrange("(p t) n -> p t n", t=PACK)[:, t, :])
             return pg
 
-        def load_wgs(t0, t1, name):
-            w = new([P, t1 - t0, S], F32, name)
+        def load_wgs(t):
+            w = new([P, S], F32, f"wgs{t}")
             for q in range(4):
-                nc.sync.dma_start(w[32 * q : 32 * (q + 1)], wgs.rearrange("(p t) j -> p t j", t=PACK)[:, t0:t1, :])
+                nc.sync.dma_start(w[32 * q : 32 * (q + 1), :], wgs.rearrange("(p t) j -> p t j", t=PACK)[:, t, :])
             return w
 
         tab_sc = new([P, 2, T], U8, "tab_sc")
@@ -93,18 +92,20 @@ def tile_list_shearer_horizon_scores_kernel(
         w1_raw = {(0, 0): load_w1(0, 0), (1, 0): load_w1(1, 0)}
         idx3 = load_list(offs3, "idx3")
         pages = {(0, 0): load_page(0, 0)}
-        wgs_first = load_wgs(0, 1, "wgs_first")
+        wgs_t = [load_wgs(0)]
         pages[0, 1] = load_page(0, 1)
-        wgs_rest = load_wgs(1, 4, "wgs_rest")
-        w4_raw.append(load_w4(1))
+        wgs_t.append(load_wgs(1))
         w1_raw[0, 1] = load_w1(0, 1)
-        w1_raw[1, 1] = load_w1(1, 1)
         pages[0, 2] = load_page(0, 2)
+        wgs_t.append(load_wgs(2))
         gains = new([P, 2, PACK], F32, "gains")
         nc.sync.dma_start(gains[:], gain.rearrange("(b p t) -> p b t", b=2, t=PACK))
+        w1_raw[1, 1] = load_w1(1, 1)
+        w4_raw.append(load_w4(1))
         pages[0, 3] = load_page(0, 3)
-        idx2 = load_list(offs2, "idx2")
+        wgs_t.append(load_wgs(3))
         pages[1, 0] = load_page(1, 0)
+        idx2 = load_list(offs2, "idx2")
         pages[1, 1] = load_page(1, 1)
         for q in range(4):
             nc.sync.dma_start(
@@ -119,9 +120,6 @@ def tile_list_shearer_horizon_scores_kernel(
         with nc.allow_non_contiguous_dma(reason="one offset for each candidate, on its partition"):
             nc.sync.dma_start(seams[:], seam.rearrange("(m p) -> p m", p=P))
 
-        def wgs_of(t):
-            return wgs_first[:, 0, :] if t == 0 else wgs_rest[:, t - 1, :]
-
         v_w, v_s = [], []
         for a in range(2):
             vw = new([P, S], U32, f"v_w{a}")
@@ -135,34 +133,36 @@ def tile_list_shearer_horizon_scores_kernel(
         for b in range(2):
             ww = new([P, 2, 2 * PASS], U8, f"w4_w{b}")
             nc.scalar.copy(
-                ww[:].bitcast(U16).rearrange("p a (t m) -> p a m t", t=PACK),
-                w4_raw[b][:].bitcast(U16).rearrange("p a (m t) -> p a m t", t=PACK),
+                ww[:].bitcast(U16).rearrange("p a (t m) -> p a t m", t=PACK),
+                w4_raw[b][:].bitcast(U16).rearrange("p a (m t) -> p a t m", t=PACK),
             )
             ws = new([P, 2, PASS], U8, f"w4_s{b}")
             nc.vector.tensor_copy(
-                ws[:].rearrange("p a (t m) -> p a m t", t=PACK),
-                w4_sc[:, :, b * PASS : (b + 1) * PASS].rearrange("p a (m t) -> p a m t", t=PACK),
+                ws[:].rearrange("p a (t m) -> p a t m", t=PACK),
+                w4_sc[:, :, b * PASS : (b + 1) * PASS].rearrange("p a (m t) -> p a t m", t=PACK),
             )
             w4_w.append(ww)
             w4_s.append(ws)
 
-        def quantise_w1(a, b, vector_share):
+        def quantise_w1(a, b):
             grouped = new([P, PACK * PASS], BF16, f"w1_bf{a}{b}")
-            dst = grouped[:].rearrange("p (t m j) -> p m j t", t=PACK, j=PACK)
-            src = w1_raw[a, b][:].rearrange("p j (m t) -> p m j t", t=PACK)
-            if vector_share:
-                nc.vector.tensor_copy(dst[:, :vector_share], src[:, :vector_share])
-            nc.scalar.copy(dst[:, vector_share:], src[:, vector_share:])
+            dst = grouped[:].rearrange("p (u v m j) -> p u m j v", u=2, v=2, j=PACK)
+            src = w1_raw[a, b][:].rearrange("p j (m u v) -> p u m j v", u=2, v=2)
+            if b == 0:
+                nc.vector.tensor_copy(dst[:, 0], src[:, 0])
+                nc.scalar.copy(dst[:, 1], src[:, 1])
+            else:
+                nc.scalar.copy(dst, src)
             codes = new([P, PASS], U32, f"w1_w{a}{b}")
             scales = new([P, PASS], U8, f"w1_s{a}{b}")
-            cuts = (0, P, PASS) if (a, b) == (1, 0) else (0, PASS)
+            cuts = (0, PASS // 2, PASS) if b == 0 else (0, PASS)
             for c0, c1 in zip(cuts, cuts[1:]):
                 nc.vector.quantize_mx(
                     codes[:, c0:c1].bitcast(FP8X4), scales[:, c0:c1], grouped[:, PACK * c0 : PACK * c1]
                 )
             return codes, scales
 
-        def product_w4(b, t):
+        def product_w4(b, t, held):
             acc = ps.tile([P, BANK], F32, name=f"acc4_{b}{t}", tag=f"bank{2 + t % 2}")
             for a in range(2):
                 nc.tensor.matmul_mx(
@@ -172,11 +172,10 @@ def tile_list_shearer_horizon_scores_kernel(
                     rhs=v_w[a][:].bitcast(FP8X4), rhs_scale=v_s[a][:],
                     start=(a == 0), stop=(a == 1),
                 )
-            held = new([P, S], F32, f"sum4_{b}{t}")
-            nc.scalar.copy(held[:], acc[:])
+            nc.scalar.copy(held, acc[:])
             return held
 
-        def refresh(b, t, w1q, h_tag=None):
+        def refresh(b, t, w1q, h=None):
             sum4 = sums4[b, t]
             acc = ps.tile([P, BANK], F32, name=f"acc1_{b}{t}", tag=f"bank{4 + t}")
             for a in range(2):
@@ -187,9 +186,10 @@ def tile_list_shearer_horizon_scores_kernel(
                     rhs=v_w[a][:].bitcast(FP8X4), rhs_scale=v_s[a][:],
                     start=(a == 0), stop=(a == 1),
                 )
-            h = new([P, S], F32, f"h{b}{t}", tag=h_tag or "h", bufs=1 if h_tag else 2)
-            nc.vector.tensor_tensor(h[:], acc[:], sum4[:], ALU.max)
-            nc.vector.tensor_tensor(pages[b, t][:].indirect(idx3[:]), h[:], wgs_of(t), ALU.mult)
+            if h is None:
+                h = new([P, S], F32, f"h{b}{t}", tag="h", bufs=2)[:]
+            nc.vector.tensor_tensor(h, acc[:], sum4, ALU.max)
+            nc.vector.tensor_tensor(pages[b, t][:].indirect(idx3[:]), h, wgs_t[t][:], ALU.mult)
 
         def quantise_x(b, half, grouped, codes, scales):
             nc.vector.quantize_mx(
@@ -198,16 +198,20 @@ def tile_list_shearer_horizon_scores_kernel(
                 grouped[:, half * BANK : (half + 1) * BANK, :].rearrange("p n t -> p (n t)"),
             )
 
-        w1q0 = [quantise_w1(a, 0, W1_VECTOR_SHARE) for a in range(2)]
-        sums4 = {(0, 0): product_w4(0, 0)}
+        w1q0 = [quantise_w1(a, 0) for a in range(2)]
+        sums4 = {(0, 0): product_w4(0, 0, new([P, S], F32, "sum4_first", tag="w1raw00")[:])}
         refresh(0, 0, w1q0)
-        sums4[0, 1] = product_w4(0, 1)
+        sum4_rest = new([P, PACK - 1, S], F32, "sum4_rest", tag="w1raw10")
+        sums4[0, 1] = product_w4(0, 1, sum4_rest[:, 0, :])
         refresh(0, 1, w1q0)
-        for b, t in ((0, 2), (0, 3), (1, 0), (1, 1), (1, 2), (1, 3)):
-            sums4[b, t] = product_w4(b, t)
-        w1q1 = [quantise_w1(a, 1, 0) for a in range(2)]
+        for t in (2, 3):
+            sums4[0, t] = product_w4(0, t, sum4_rest[:, t - 1, :])
+        sum4_second = new([P, PACK, S], F32, "sum4_second")
+        for t in range(PACK):
+            sums4[1, t] = product_w4(1, t, sum4_second[:, t, :])
+        w1q1 = [quantise_w1(a, 1) for a in range(2)]
         refresh(0, 2, w1q0)
-        refresh(0, 3, w1q0, h_tag="w1_bf11")
+        refresh(0, 3, w1q0, new([P, S], F32, "h03", tag="w1_bf11")[:])
 
         planes = new([P, PACK, T2], BF16, "x_planes", tag="w1raw11")
         for t in range(PACK):
@@ -225,61 +229,71 @@ def tile_list_shearer_horizon_scores_kernel(
         refresh(1, 0, w1q1)
         refresh(1, 1, w1q1)
 
-        def gather_candidates(part, words_tag, scales_tag):
-            lst = idx2[:, 16 * part : 16 * (part + 1)]
-            words = new([P, 2, S2 // 2], U32, f"v2_w{part}", tag=words_tag)
+        def gather_candidates(first, count, words_tag):
+            lst = idx2[:, first // 16 : (first + count) // 16]
+            words = new([P, 2, count], U32, f"v2_w{first}", tag=words_tag)
             for a in range(2):
                 nc.vector.tensor_copy(words[:, a, :], tab2_w[a][:].bitcast(U32).indirect(lst))
-            scales = new([P, S2 // 2], U8, f"v2_s{part}", tag=scales_tag)
-            nc.vector.tensor_copy(scales[:], tab2_sc[:].indirect(lst))
-            return words, scales
+            return words
 
-        v2 = [gather_candidates(0, None, None)]
+        v2_first = gather_candidates(0, P, None)
+        v2_s = new([P, S2], U8, "v2_s")
+        nc.vector.tensor_copy(v2_s[:], tab2_sc[:].indirect(idx2[:]))
         for half in range(2):
             quantise_x(0, half, x_bf0, x_w[0], x_s[0])
 
         x_bf1 = new([P, T2, PACK], BF16, "x_bf1", tag="w1raw11")
         for t in range(2):
             nc.scalar.activation(x_bf1[:, :, t], pages[1, t][:], ACT.Copy, scale=gains[:, 1, t : t + 1])
-        refresh(1, 2, w1q1, h_tag="x_bf0")
+        h_last = new([P, 2, S], F32, "h_last", tag="x_bf0")
+        refresh(1, 2, w1q1, h_last[:, 0, :])
         gain_now = new([P, 1], F32, "gain_now")
         nc.scalar.copy(gain_now[:], gains[:, 1, 2:3])
         nc.scalar.activation(x_bf1[:, :BANK, 2], pages[1, 2][:, :BANK], ACT.Copy, scale=gain_now[:])
-        nc.scalar.copy(gain_now[:], gains[:, 1, 3:4])
-        nc.scalar.activation(x_bf1[:, BANK:, 2], pages[1, 2][:, BANK:], ACT.Copy, scale=gains[:, 1, 2:3])
-        refresh(1, 3, w1q1)
-        nc.vector.tensor_scalar(x_bf1[:, :BANK, 3], pages[1, 3][:, :BANK], gain_now[:], None, ALU.mult)
+        gain_last = new([P, 2], F32, "gain_last", tag="gain_now")
+        nc.scalar.copy(gain_last[:], gains[:, 1, 2:4])
+        nc.scalar.activation(x_bf1[:, BANK:, 2], pages[1, 2][:, BANK:], ACT.Copy, scale=gain_last[:, 0:1])
+        refresh(1, 3, w1q1, h_last[:, 1, :])
+        nc.vector.tensor_scalar(x_bf1[:, :BANK, 3], pages[1, 3][:, :BANK], gain_last[:, 1:2], None, ALU.mult)
         nc.scalar.activation(x_bf1[:, BANK:, 3], pages[1, 3][:, BANK:], ACT.Copy, scale=gains[:, 1, 3:4])
         for half in range(2):
             quantise_x(1, half, x_bf1, x_w[1], x_s[1])
-        v2.append(gather_candidates(1, "gain_now", "page13"))
+        v2_rest = gather_candidates(P, S2 - P, "w1raw11")
 
+        scores = []
         for m in range(S2 // P):
             rows = slice(m * P, (m + 1) * P)
             e = new([P, T2], F32, f"e{m}", tag=f"page0{m}")
-            v2_w, v2_s = v2[m // 2]
-            cand = slice((m % 2) * P, (m % 2 + 1) * P)
+            v2_w = v2_first if m == 0 else v2_rest[:, :, (m - 1) * P : m * P]
+            scores.append(e)
             for half in range(2):
                 cols = slice(half * BANK, (half + 1) * BANK)
                 acc = ps.tile([P, BANK], F32, name=f"acc_e{m}{half}", tag=f"bank{2 * m + half}")
                 for b in range(2):
                     nc.tensor.matmul_mx(
                         acc[:],
-                        lhsT=v2_w[:, b, cand].bitcast(FP8X4), lhsT_scale=v2_s[4 * b :, cand],
+                        lhsT=v2_w[:, b, :].bitcast(FP8X4), lhsT_scale=v2_s[4 * b :, rows],
                         rhs=x_w[b][:, cols].bitcast(FP8X4), rhs_scale=x_s[b][:, cols],
                         start=(b == 0), stop=(b == 1),
                     )
                 nc.scalar.copy(e[:, cols], acc[:])
-            pieces = 2
-            width = PAIRS // pieces
-            for piece in range(pieces):
-                lst = slice(piece * width // 16, (piece + 1) * width // 16)
-                floor = new([P, width], F32, f"floor{m}{piece}", tag="floor", bufs=4)
-                nc.vector.tensor_copy(floor[:], e[:].indirect(p2[:, lst]))
-                diff = new([P, width], F32, f"diff{m}{piece}", tag="diff", bufs=4)
-                nc.vector.tensor_tensor(diff[:], e[:].indirect(p1[:, lst]), floor[:], ALU.subtract)
-                size = new([P, width], F32, f"size{m}{piece}", tag="size", bufs=4)
-                nc.scalar.activation(size[:], diff[:], ACT.Abs)
-                res = new([P, width], F32, f"res{m}{piece}", tag="res", bufs=4)
-                nc.scalar.activation(res[:], size[:], ACT.Identity, bias=seams[:, m : m + 1])
-                nc.sync.dma_start(out[rows, piece * width : (piece + 1) * width], res[:])
+
+        for m, e in enumerate(scores):
+            rows = slice(m * P, (m + 1) * P)
+            floor = new([P, PAIRS], F32, f"floor{m}")
+            diff = new([P, PAIRS], F32, f"diff{m}")
+            res = new([P, PAIRS], F32, f"res{m}")
+            last = m == len(scores) - 1
+            cuts = (0, 256, PAIRS)
+            for c0, c1 in zip(cuts, cuts[1:]):
+                nc.vector.tensor_copy(floor[:, c0:c1], e[:].indirect(p2[:, c0 // 16 : c1 // 16]))
+            for c0, c1 in zip(cuts, cuts[1:]):
+                nc.vector.tensor_tensor(
+                    diff[:, c0:c1], e[:].indirect(p1[:, c0 // 16 : c1 // 16]), floor[:, c0:c1], ALU.subtract
+                )
+            cuts = cuts if last else (0, PAIRS)
+            for c0, c1 in zip(cuts, cuts[1:]):
+                size = new([P, c1 - c0], F32, f"size{m}_{c0}", tag="size")
+                nc.scalar.activation(size[:], diff[:, c0:c1], ACT.Abs)
+                nc.scalar.activation(res[:, c0:c1], size[:], ACT.Identity, bias=seams[:, m : m + 1])
+                nc.sync.dma_start(out[rows, c0:c1], res[:, c0:c1])

@@ -1,6 +1,7 @@
 from contextlib import ExitStack
 
 import concourse.mybir as mybir
+from concourse.masks import make_identity
 
 K, H, T, S, T2, T3, S2, PAIRS = 1024, 1024, 2048, 512, 1024, 2048, 512, 512
 FLOPS = 2 * K * H * S * 2 + 2 * H * S2 * T2
@@ -20,6 +21,8 @@ P = 128
 PACK = 4
 PASS = P * PACK
 BANK = 512
+WEAVE_VECTOR = 640
+LAST_SCALAR = 320
 
 
 def tile_list_shearer_horizon_scores_kernel(
@@ -44,11 +47,9 @@ def tile_list_shearer_horizon_scores_kernel(
             nc.sync.dma_start(t[:], src[a].rearrange("p t i -> p (t i)").bitcast(I32))
             return t
 
-        def load_w1(a, b):
-            t = new([P, PACK, PASS], F32, f"w1raw{a}{b}")
-            nc.sync.dma_start(
-                t[:], w1[a * PASS : (a + 1) * PASS, b * PASS : (b + 1) * PASS].rearrange("(p j) c -> p j c", j=PACK)
-            )
+        def load_w1(a, c0, c1):
+            t = new([P, PACK, c1 - c0], F32, f"w1raw{a}_{c0}")
+            nc.sync.dma_start(t[:], w1[a * PASS : (a + 1) * PASS, c0:c1].rearrange("(p j) c -> p j c", j=PACK))
             return t
 
         def load_w4(b):
@@ -61,7 +62,10 @@ def tile_list_shearer_horizon_scores_kernel(
 
         def load_page(b, t):
             pg = new([P, T2], F32, f"page{b}{t}")
-            nc.sync.dma_start(pg[:], page0[b * PASS : (b + 1) * PASS, :].rearrange("(p t) n -> p t n", t=PACK)[:, t, :])
+            if b == 0:
+                nc.sync.dma_start(pg[:], page0[t * P : (t + 1) * P, :])
+            else:
+                nc.sync.dma_start(pg[:], page0[PASS:, :].rearrange("(p t) n -> p t n", t=PACK)[:, t, :])
             return pg
 
         def load_wgs(t):
@@ -89,36 +93,47 @@ def tile_list_shearer_horizon_scores_kernel(
             nc.sync.dma_start(
                 w4_sc[r:P:32].bitcast(I32), w4_scales.bitcast(I32).rearrange("a (q r) t -> r q a t", r=4)[r]
             )
-        w1_raw = {(0, 0): load_w1(0, 0), (1, 0): load_w1(1, 0)}
+        w1_head = [load_w1(a, 0, 2 * P) for a in range(2)]
         idx3 = load_list(offs3, "idx3")
         pages = {(0, 0): load_page(0, 0)}
-        wgs_t = [load_wgs(0)]
+        wgs_plain = new([P, S], F32, "wgs_plain")
+        nc.sync.dma_start(wgs_plain[:], wgs)
+        w1_next = [load_w1(a, 2 * P, PASS) for a in range(2)]
+        p1 = load_list(pos1, "p1")
         pages[0, 1] = load_page(0, 1)
-        wgs_t.append(load_wgs(1))
-        w1_raw[0, 1] = load_w1(0, 1)
+        gains0 = new([P, PACK], F32, "gains0")
+        with nc.allow_non_contiguous_dma(reason="one gain for each row, on its partition"):
+            nc.sync.dma_start(gains0[:], gain[:PASS].rearrange("(c q) -> q c", q=P))
+        w1_last = [load_w1(0, PASS, H)]
         pages[0, 2] = load_page(0, 2)
-        wgs_t.append(load_wgs(2))
-        gains = new([P, 2, PACK], F32, "gains")
-        nc.sync.dma_start(gains[:], gain.rearrange("(b p t) -> p b t", b=2, t=PACK))
-        w1_raw[1, 1] = load_w1(1, 1)
+        w1_last.append(load_w1(1, PASS, H))
         w4_raw.append(load_w4(1))
-        pages[0, 3] = load_page(0, 3)
-        wgs_t.append(load_wgs(3))
-        pages[1, 0] = load_page(1, 0)
+        p2 = load_list(pos2, "p2")
         idx2 = load_list(offs2, "idx2")
+        gains1 = new([P, PACK], F32, "gains1")
+        nc.sync.dma_start(gains1[:], gain[PASS:].rearrange("(p t) -> p t", t=PACK))
+        pages[0, 3] = load_page(0, 3)
+        pages[1, 0] = load_page(1, 0)
+        wgs_t = [load_wgs(0)]
         pages[1, 1] = load_page(1, 1)
+        wgs_t.append(load_wgs(1))
         for q in range(4):
             nc.sync.dma_start(
                 tab2_sc[32 * q : 32 * q + 8, :].bitcast(I32), tab2_scales.bitcast(I32)[:, 4 * q : 4 * q + 4, :]
             )
         tab2_w = [load_words(tab2_words, a, f"tab2_w{a}") for a in range(2)]
         pages[1, 2] = load_page(1, 2)
+        wgs_t.append(load_wgs(2))
         pages[1, 3] = load_page(1, 3)
-        p1 = load_list(pos1, "p1")
-        p2 = load_list(pos2, "p2")
+        wgs_t.append(load_wgs(3))
         seams = new([P, S2 // P], F32, "seams")
         with nc.allow_non_contiguous_dma(reason="one offset for each candidate, on its partition"):
             nc.sync.dma_start(seams[:], seam.rearrange("(m p) -> p m", p=P))
+
+        ident_words = new([P, P], F32, "ident_words")
+        make_identity(nc, ident_words[:])
+        ident_bf = new([P, P], BF16, "ident_bf")
+        make_identity(nc, ident_bf[:])
 
         v_w, v_s = [], []
         for a in range(2):
@@ -129,38 +144,50 @@ def tile_list_shearer_horizon_scores_kernel(
             v_w.append(vw)
             v_s.append(vs)
 
-        w4_w, w4_s = [], []
-        for b in range(2):
-            ww = new([P, 2, 2 * PASS], U8, f"w4_w{b}")
-            nc.scalar.copy(
-                ww[:].bitcast(U16).rearrange("p a (t m) -> p a t m", t=PACK),
-                w4_raw[b][:].bitcast(U16).rearrange("p a (m t) -> p a t m", t=PACK),
-            )
-            ws = new([P, 2, PASS], U8, f"w4_s{b}")
-            nc.vector.tensor_copy(
-                ws[:].rearrange("p a (t m) -> p a t m", t=PACK),
-                w4_sc[:, :, b * PASS : (b + 1) * PASS].rearrange("p a (m t) -> p a t m", t=PACK),
-            )
-            w4_w.append(ww)
-            w4_s.append(ws)
+        w4_dealt = new([P, 2, 2 * PASS], U8, "w4_dealt")
+        nc.scalar.copy(
+            w4_dealt[:].bitcast(U16).rearrange("p a (t m) -> p a t m", t=PACK),
+            w4_raw[1][:].bitcast(U16).rearrange("p a (m t) -> p a t m", t=PACK),
+        )
+        w4_sc_dealt = new([P, 2, PASS], U8, "w4_sc_dealt")
+        nc.vector.tensor_copy(
+            w4_sc_dealt[:].rearrange("p a (t m) -> p a t m", t=PACK),
+            w4_sc[:, :, PASS:].rearrange("p a (m t) -> p a t m", t=PACK),
+        )
+        w4_w = [w4_raw[0], w4_dealt]
+        w4_s = [w4_sc, w4_sc_dealt]
 
-        def quantise_w1(a, b):
-            grouped = new([P, PACK * PASS], BF16, f"w1_bf{a}{b}")
-            dst = grouped[:].rearrange("p (u v m j) -> p u m j v", u=2, v=2, j=PACK)
-            src = w1_raw[a, b][:].rearrange("p j (m u v) -> p u m j v", u=2, v=2)
-            if b == 0:
-                nc.vector.tensor_copy(dst[:, 0], src[:, 0])
-                nc.scalar.copy(dst[:, 1], src[:, 1])
-            else:
-                nc.scalar.copy(dst, src)
-            codes = new([P, PASS], U32, f"w1_w{a}{b}")
-            scales = new([P, PASS], U8, f"w1_s{a}{b}")
-            cuts = (0, PASS // 2, PASS) if b == 0 else (0, PASS)
-            for c0, c1 in zip(cuts, cuts[1:]):
-                nc.vector.quantize_mx(
-                    codes[:, c0:c1].bitcast(FP8X4), scales[:, c0:c1], grouped[:, PACK * c0 : PACK * c1]
-                )
-            return codes, scales
+        w1_w = [[new([P, PASS], U32, f"w1_w{a}{b}") for a in range(2)] for b in range(2)]
+        w1_s = [[new([P, PASS], U8, f"w1_s{a}{b}") for a in range(2)] for b in range(2)]
+
+        def quantise_w1(a, b, c0, c1, grouped):
+            nc.vector.quantize_mx(w1_w[b][a][:, c0:c1].bitcast(FP8X4), w1_s[b][a][:, c0:c1], grouped)
+
+        def weave_plain(raw, name):
+            grouped = new([P, PACK * 2 * P], BF16, name)
+            dst = grouped[:].rearrange("p (c i j) -> p c j i", i=4, j=PACK)
+            src = raw[:].rearrange("p j (c i) -> p c j i", i=4)
+            return grouped, dst, src
+
+        def w1_first(a):
+            grouped, dst, src = weave_plain(w1_head[a], f"w1_bf_head{a}")
+            nc.vector.tensor_copy(dst[:, : P // 4], src[:, : P // 4])
+            nc.scalar.copy(dst[:, P // 4 :], src[:, P // 4 :])
+            quantise_w1(a, 0, 0, P, grouped[:, :PASS])
+            quantise_w1(a, 0, P, 2 * P, grouped[:, PASS:])
+
+        def w1_second(a):
+            grouped, dst, src = weave_plain(w1_next[a], f"w1_bf_next{a}")
+            nc.scalar.copy(dst, src)
+            quantise_w1(a, 0, 2 * P, PASS, grouped[:])
+
+        def w1_dealt(a):
+            grouped = new([P, PACK * PASS], BF16, f"w1_bf_last{a}")
+            nc.scalar.copy(
+                grouped[:].rearrange("p (u v m j) -> p u m j v", u=2, v=2, j=PACK),
+                w1_last[a][:].rearrange("p j (m u v) -> p u m j v", u=2, v=2),
+            )
+            quantise_w1(a, 1, 0, PASS, grouped[:])
 
         def product_w4(b, t, held):
             acc = ps.tile([P, BANK], F32, name=f"acc4_{b}{t}", tag=f"bank{2 + t % 2}")
@@ -175,21 +202,21 @@ def tile_list_shearer_horizon_scores_kernel(
             nc.scalar.copy(held, acc[:])
             return held
 
-        def refresh(b, t, w1q, h=None):
+        def refresh(b, t, h=None):
             sum4 = sums4[b, t]
             acc = ps.tile([P, BANK], F32, name=f"acc1_{b}{t}", tag=f"bank{4 + t}")
             for a in range(2):
                 nc.tensor.matmul_mx(
                     acc[:],
-                    lhsT=w1q[a][0][:, P * t : P * (t + 1)].bitcast(FP8X4),
-                    lhsT_scale=w1q[a][1][:, P * t : P * (t + 1)],
+                    lhsT=w1_w[b][a][:, P * t : P * (t + 1)].bitcast(FP8X4),
+                    lhsT_scale=w1_s[b][a][:, P * t : P * (t + 1)],
                     rhs=v_w[a][:].bitcast(FP8X4), rhs_scale=v_s[a][:],
                     start=(a == 0), stop=(a == 1),
                 )
             if h is None:
                 h = new([P, S], F32, f"h{b}{t}", tag="h", bufs=2)[:]
             nc.vector.tensor_tensor(h, acc[:], sum4, ALU.max)
-            nc.vector.tensor_tensor(pages[b, t][:].indirect(idx3[:]), h, wgs_t[t][:], ALU.mult)
+            nc.vector.tensor_tensor(pages[b, t][:].indirect(idx3[:]), h, wgs_t[t][:] if b else wgs_plain[:], ALU.mult)
 
         def quantise_x(b, half, grouped, codes, scales):
             nc.vector.quantize_mx(
@@ -198,36 +225,57 @@ def tile_list_shearer_horizon_scores_kernel(
                 grouped[:, half * BANK : (half + 1) * BANK, :].rearrange("p n t -> p (n t)"),
             )
 
-        w1q0 = [quantise_w1(a, 0) for a in range(2)]
-        sums4 = {(0, 0): product_w4(0, 0, new([P, S], F32, "sum4_first", tag="w1raw00")[:])}
-        refresh(0, 0, w1q0)
-        sum4_rest = new([P, PACK - 1, S], F32, "sum4_rest", tag="w1raw10")
-        sums4[0, 1] = product_w4(0, 1, sum4_rest[:, 0, :])
-        refresh(0, 1, w1q0)
+        w1_first(0)
+        w1_first(1)
+        sums4 = {(0, 0): product_w4(0, 0, new([P, S], F32, "sum4_first", tag="w1raw0_0")[:])}
+        refresh(0, 0)
+        sums4[0, 1] = product_w4(0, 1, new([P, S], F32, "sum4_second", tag="w1raw1_0")[:])
+        refresh(0, 1)
+        w1_second(0)
+        w1_second(1)
+        sum4_third = new([P, 2, S], F32, "sum4_third", tag="w1raw1_256")
         for t in (2, 3):
-            sums4[0, t] = product_w4(0, t, sum4_rest[:, t - 1, :])
-        sum4_second = new([P, PACK, S], F32, "sum4_second")
-        for t in range(PACK):
-            sums4[1, t] = product_w4(1, t, sum4_second[:, t, :])
-        w1q1 = [quantise_w1(a, 1) for a in range(2)]
-        refresh(0, 2, w1q0)
-        refresh(0, 3, w1q0, new([P, S], F32, "h03", tag="w1_bf11")[:])
+            sums4[0, t] = product_w4(0, t, sum4_third[:, t - 2, :])
+        refresh(0, 2)
+        w1_dealt(0)
+        w1_dealt(1)
+        sum4_last = new([P, PACK, S], F32, "sum4_last")
+        for t in range(2):
+            sums4[1, t] = product_w4(1, t, sum4_last[:, t, :])
+        refresh(0, 3, new([P, S], F32, "h03", tag="w1_bf_last1")[:])
 
-        planes = new([P, PACK, T2], BF16, "x_planes", tag="w1raw11")
-        for t in range(PACK):
-            nc.scalar.activation(planes[:, t, :], pages[0, t][:], ACT.Copy, scale=gains[:, 0, t : t + 1])
-        x_bf0 = new([P, T2, PACK], BF16, "x_bf0")
-        x_w = [new([P, T2], U32, f"x_w{b}") for b in range(2)]
-        x_s = [new([P, T2], U8, f"x_s{b}") for b in range(2)]
-        for half in range(2):
-            cols = slice(half * BANK, (half + 1) * BANK)
+        h_pair = new([P, 2, S], F32, "h_pair", tag="w1_bf_last1")
+        refresh(1, 0, h_pair[:, 0, :])
+        refresh(1, 1, h_pair[:, 1, :])
+
+        row_pairs = new([P, T2 // P, 2, P], F32, "row_pairs", tag="w1raw0_512")
+        late = new([P, PACK - 1, T2], BF16, "x_plane_late", tag="w1raw1_512")
+        planes = [new([P, T2], BF16, "x_plane0")[:]] + [late[:, c, :] for c in range(PACK - 1)]
+        for c in range(PACK):
+            nc.scalar.activation(planes[c], pages[0, c][:], ACT.Copy, scale=gains0[:, c : c + 1])
+            turned = ps.tile([P, T2 // P, P], BF16, name=f"turned{c}", tag=f"bank{c % 2}")
+            for k in range(T2 // P):
+                nc.tensor.transpose(turned[:, k, :], planes[c][:, k * P : (k + 1) * P], ident_bf[:])
             nc.scalar.copy(
-                x_bf0[:, cols, :].rearrange("p (c i) t -> p c t i", i=4),
-                planes[:, :, cols].rearrange("p t (c i) -> p c t i", i=4),
+                row_pairs[:, :, :, 32 * c : 32 * (c + 1)], turned[:].bitcast(F32).rearrange("p k (w u) -> p k u w", u=2)
             )
+        x_bf0 = new([P, T2, PACK], BF16, "x_bf0")
+        x_pairs = x_bf0[:].bitcast(F32)
+        for g in range(T2 // (2 * P)):
+            back = ps.tile([P, 2, 2, P], F32, name=f"back{g}", tag=f"bank{g % 2}")
+            for k in range(2):
+                for u in range(2):
+                    nc.tensor.transpose(back[:, k, u, :], row_pairs[:, 2 * g + k, u, :], ident_words[:])
+            nc.scalar.copy(
+                x_pairs[:, 2 * P * g : 2 * P * (g + 1), :].rearrange("p (k n) u -> p k n u", k=2),
+                back[:].rearrange("p k u n -> p k n u"),
+            )
+        x_s = [new([P, T2], U8, "x_s0", tag="tab2_sc"), new([P, T2], U8, "x_s1")]
 
-        refresh(1, 0, w1q1)
-        refresh(1, 1, w1q1)
+        x_w = [new([P, T2], U32, "x_w0", tag="w1_bf_last1"), new([P, T2], U32, "x_w1")]
+
+        for t in (2, 3):
+            sums4[1, t] = product_w4(1, t, sum4_last[:, t, :])
 
         def gather_candidates(first, count, words_tag):
             lst = idx2[:, first // 16 : (first + count) // 16]
@@ -242,23 +290,23 @@ def tile_list_shearer_horizon_scores_kernel(
         for half in range(2):
             quantise_x(0, half, x_bf0, x_w[0], x_s[0])
 
-        x_bf1 = new([P, T2, PACK], BF16, "x_bf1", tag="w1raw11")
+        x_bf1 = new([P, T2, PACK], BF16, "x_bf1", tag="w1raw0_512")
         for t in range(2):
-            nc.scalar.activation(x_bf1[:, :, t], pages[1, t][:], ACT.Copy, scale=gains[:, 1, t : t + 1])
+            nc.scalar.activation(x_bf1[:, :, t], pages[1, t][:], ACT.Copy, scale=gains1[:, t : t + 1])
         h_last = new([P, 2, S], F32, "h_last", tag="x_bf0")
-        refresh(1, 2, w1q1, h_last[:, 0, :])
+        refresh(1, 2, h_last[:, 0, :])
         gain_now = new([P, 1], F32, "gain_now")
-        nc.scalar.copy(gain_now[:], gains[:, 1, 2:3])
-        nc.scalar.activation(x_bf1[:, :BANK, 2], pages[1, 2][:, :BANK], ACT.Copy, scale=gain_now[:])
+        nc.scalar.copy(gain_now[:], gains1[:, 2:3])
+        nc.scalar.activation(x_bf1[:, :WEAVE_VECTOR, 2], pages[1, 2][:, :WEAVE_VECTOR], ACT.Copy, scale=gain_now[:])
         gain_last = new([P, 2], F32, "gain_last", tag="gain_now")
-        nc.scalar.copy(gain_last[:], gains[:, 1, 2:4])
-        nc.scalar.activation(x_bf1[:, BANK:, 2], pages[1, 2][:, BANK:], ACT.Copy, scale=gain_last[:, 0:1])
-        refresh(1, 3, w1q1, h_last[:, 1, :])
-        nc.vector.tensor_scalar(x_bf1[:, :BANK, 3], pages[1, 3][:, :BANK], gain_last[:, 1:2], None, ALU.mult)
-        nc.scalar.activation(x_bf1[:, BANK:, 3], pages[1, 3][:, BANK:], ACT.Copy, scale=gains[:, 1, 3:4])
+        nc.scalar.copy(gain_last[:], gains1[:, 2:4])
+        nc.scalar.activation(x_bf1[:, WEAVE_VECTOR:, 2], pages[1, 2][:, WEAVE_VECTOR:], ACT.Copy, scale=gain_last[:, 0:1])
+        refresh(1, 3, h_last[:, 1, :])
+        nc.vector.tensor_scalar(x_bf1[:, :WEAVE_VECTOR, 3], pages[1, 3][:, :WEAVE_VECTOR], gain_last[:, 1:2], None, ALU.mult)
+        nc.scalar.activation(x_bf1[:, WEAVE_VECTOR:, 3], pages[1, 3][:, WEAVE_VECTOR:], ACT.Copy, scale=gains1[:, 3:4])
         for half in range(2):
             quantise_x(1, half, x_bf1, x_w[1], x_s[1])
-        v2_rest = gather_candidates(P, S2 - P, "w1raw11")
+        v2_rest = gather_candidates(P, S2 - P, "w1raw0_512")
 
         scores = []
         for m in range(S2 // P):
@@ -284,16 +332,19 @@ def tile_list_shearer_horizon_scores_kernel(
             diff = new([P, PAIRS], F32, f"diff{m}")
             res = new([P, PAIRS], F32, f"res{m}")
             last = m == len(scores) - 1
-            cuts = (0, 256, PAIRS)
+            cuts = (0, LAST_SCALAR if last else PAIRS // 2, PAIRS)
             for c0, c1 in zip(cuts, cuts[1:]):
                 nc.vector.tensor_copy(floor[:, c0:c1], e[:].indirect(p2[:, c0 // 16 : c1 // 16]))
             for c0, c1 in zip(cuts, cuts[1:]):
                 nc.vector.tensor_tensor(
                     diff[:, c0:c1], e[:].indirect(p1[:, c0 // 16 : c1 // 16]), floor[:, c0:c1], ALU.subtract
                 )
-            cuts = cuts if last else (0, PAIRS)
-            for c0, c1 in zip(cuts, cuts[1:]):
-                size = new([P, c1 - c0], F32, f"size{m}_{c0}", tag="size")
-                nc.scalar.activation(size[:], diff[:, c0:c1], ACT.Abs)
-                nc.scalar.activation(res[:, c0:c1], size[:], ACT.Identity, bias=seams[:, m : m + 1])
-                nc.sync.dma_start(out[rows, c0:c1], res[:, c0:c1])
+            width = LAST_SCALAR if last else PAIRS
+            size = new([P, width], F32, f"size{m}", tag="size")
+            nc.scalar.activation(size[:], diff[:, :width], ACT.Abs)
+            nc.scalar.activation(res[:, :width], size[:], ACT.Identity, bias=seams[:, m : m + 1])
+            if last:
+                size_end = new([P, PAIRS - width], F32, "size_end")
+                nc.vector.scalar_tensor_tensor(size_end[:], diff[:, width:], -1.0, diff[:, width:], ALU.mult, ALU.max)
+                nc.vector.tensor_scalar(res[:, width:], size_end[:], seams[:, m : m + 1], None, ALU.add)
+            nc.sync.dma_start(out[rows, :], res[:])

from contextlib import ExitStack

import concourse.mybir as mybir
from concourse.masks import make_identity

K, H, T, S, T2, T3, S2, PAIRS = 1024, 1024, 2048, 512, 1024, 2048, 512, 512
FLOPS = 2 * K * H * S * 2 + 2 * H * S2 * T2

F32 = mybir.dt.float32
BF16 = mybir.dt.bfloat16
I32 = mybir.dt.int32
U32 = mybir.dt.uint32
U16 = mybir.dt.uint16
U8 = mybir.dt.uint8
FP8X4 = mybir.dt.float8_e4m3fn_x4
FP4X4 = mybir.dt.float4_e2m1fn_x4
ALU = mybir.AluOpType
ACT = mybir.ActivationFunctionType

P = 128
PACK = 4
PASS = P * PACK
BANK = 512
WEAVE_VECTOR = 640
LAST_SCALAR = 320


def tile_list_shearer_horizon_scores_kernel(
    tc, tab_words, tab_scales, tab2_words, tab2_scales, w1, w4_words, w4_scales,
    page0, wgs, gain, seam, offs, offs2, offs3, pos1, pos2, out,
):
    nc = tc.nc
    with ExitStack() as ctx:
        sb = ctx.enter_context(tc.tile_pool(name="sb", bufs=1))
        ps = ctx.enter_context(tc.psum_pool(name="ps", bufs=1))

        def new(shape, dtype, name, tag=None, bufs=1):
            return sb.tile(shape, dtype, name=name, tag=tag or name, bufs=bufs, align_bytes=64)

        def load_list(src, name):
            t = new([P, 32], U16, name)
            nc.sync.dma_start(t[:], src)
            return t

        def load_words(src, a, name):
            t = new([P, T], I32, name)
            nc.sync.dma_start(t[:], src[a].rearrange("p t i -> p (t i)").bitcast(I32))
            return t

        def load_w1(a, c0, c1):
            t = new([P, PACK, c1 - c0], F32, f"w1raw{a}_{c0}")
            nc.sync.dma_start(t[:], w1[a * PASS : (a + 1) * PASS, c0:c1].rearrange("(p j) c -> p j c", j=PACK))
            return t

        def load_w4(b):
            t = new([P, 2, 2 * PASS], U8, f"w4_raw{b}")
            nc.sync.dma_start(
                t[:].bitcast(I32),
                w4_words[:, :, 2 * PASS * b : 2 * PASS * (b + 1)].bitcast(I32).rearrange("a p c -> p a c"),
            )
            return t

        def load_page(b, t):
            pg = new([P, T2], F32, f"page{b}{t}")
            if b == 0:
                nc.sync.dma_start(pg[:], page0[t * P : (t + 1) * P, :])
            else:
                nc.sync.dma_start(pg[:], page0[PASS:, :].rearrange("(p t) n -> p t n", t=PACK)[:, t, :])
            return pg

        def load_wgs(t):
            w = new([P, S], F32, f"wgs{t}")
            for q in range(4):
                nc.sync.dma_start(w[32 * q : 32 * (q + 1), :], wgs.rearrange("(p t) j -> p t j", t=PACK)[:, t, :])
            return w

        tab_sc = new([P, 2, T], U8, "tab_sc")
        nc.vector.memset(tab_sc[:].rearrange("p a t -> p (a t)").bitcast(I32), 0)
        w4_sc = new([P, 2, H], U8, "w4_sc")
        nc.gpsimd.memset(w4_sc[:].rearrange("p a t -> p (a t)").bitcast(I32), 0)
        tab2_sc = new([P, T3], U8, "tab2_sc")
        nc.gpsimd.memset(tab2_sc[:].bitcast(I32), 0)

        tab_w = [load_words(tab_words, 0, "tab_w0")]
        idx = load_list(offs, "idx")
        for r in range(4):
            nc.sync.dma_start(
                tab_sc[r:P:32].bitcast(I32), tab_scales.bitcast(I32).rearrange("a (q r) t -> r q a t", r=4)[r]
            )
        tab_w.append(load_words(tab_words, 1, "tab_w1"))
        w4_raw = [load_w4(0)]
        for r in range(4):
            nc.sync.dma_start(
                w4_sc[r:P:32].bitcast(I32), w4_scales.bitcast(I32).rearrange("a (q r) t -> r q a t", r=4)[r]
            )
        w1_head = [load_w1(a, 0, 2 * P) for a in range(2)]
        idx3 = load_list(offs3, "idx3")
        pages = {(0, 0): load_page(0, 0)}
        wgs_plain = new([P, S], F32, "wgs_plain")
        nc.sync.dma_start(wgs_plain[:], wgs)
        w1_next = [load_w1(a, 2 * P, PASS) for a in range(2)]
        p1 = load_list(pos1, "p1")
        pages[0, 1] = load_page(0, 1)
        gains0 = new([P, PACK], F32, "gains0")
        with nc.allow_non_contiguous_dma(reason="one gain for each row, on its partition"):
            nc.sync.dma_start(gains0[:], gain[:PASS].rearrange("(c q) -> q c", q=P))
        w1_last = [load_w1(0, PASS, H)]
        pages[0, 2] = load_page(0, 2)
        w1_last.append(load_w1(1, PASS, H))
        w4_raw.append(load_w4(1))
        p2 = load_list(pos2, "p2")
        idx2 = load_list(offs2, "idx2")
        gains1 = new([P, PACK], F32, "gains1")
        nc.sync.dma_start(gains1[:], gain[PASS:].rearrange("(p t) -> p t", t=PACK))
        pages[0, 3] = load_page(0, 3)
        pages[1, 0] = load_page(1, 0)
        wgs_t = [load_wgs(0)]
        pages[1, 1] = load_page(1, 1)
        wgs_t.append(load_wgs(1))
        for q in range(4):
            nc.sync.dma_start(
                tab2_sc[32 * q : 32 * q + 8, :].bitcast(I32), tab2_scales.bitcast(I32)[:, 4 * q : 4 * q + 4, :]
            )
        tab2_w = [load_words(tab2_words, a, f"tab2_w{a}") for a in range(2)]
        pages[1, 2] = load_page(1, 2)
        wgs_t.append(load_wgs(2))
        pages[1, 3] = load_page(1, 3)
        wgs_t.append(load_wgs(3))
        seams = new([P, S2 // P], F32, "seams")
        with nc.allow_non_contiguous_dma(reason="one offset for each candidate, on its partition"):
            nc.sync.dma_start(seams[:], seam.rearrange("(m p) -> p m", p=P))

        ident_words = new([P, P], F32, "ident_words")
        make_identity(nc, ident_words[:])
        ident_bf = new([P, P], BF16, "ident_bf")
        make_identity(nc, ident_bf[:])

        v_w, v_s = [], []
        for a in range(2):
            vw = new([P, S], U32, f"v_w{a}")
            nc.vector.tensor_copy(vw[:], tab_w[a][:].bitcast(U32).indirect(idx[:]))
            vs = new([P, S], U8, f"v_s{a}")
            nc.vector.tensor_copy(vs[:], tab_sc[:, a, :].indirect(idx[:]))
            v_w.append(vw)
            v_s.append(vs)

        w4_dealt = new([P, 2, 2 * PASS], U8, "w4_dealt")
        nc.scalar.copy(
            w4_dealt[:].bitcast(U16).rearrange("p a (t m) -> p a t m", t=PACK),
            w4_raw[1][:].bitcast(U16).rearrange("p a (m t) -> p a t m", t=PACK),
        )
        w4_sc_dealt = new([P, 2, PASS], U8, "w4_sc_dealt")
        nc.vector.tensor_copy(
            w4_sc_dealt[:].rearrange("p a (t m) -> p a t m", t=PACK),
            w4_sc[:, :, PASS:].rearrange("p a (m t) -> p a t m", t=PACK),
        )
        w4_w = [w4_raw[0], w4_dealt]
        w4_s = [w4_sc, w4_sc_dealt]

        w1_w = [[new([P, PASS], U32, f"w1_w{a}{b}") for a in range(2)] for b in range(2)]
        w1_s = [[new([P, PASS], U8, f"w1_s{a}{b}") for a in range(2)] for b in range(2)]

        def quantise_w1(a, b, c0, c1, grouped):
            nc.vector.quantize_mx(w1_w[b][a][:, c0:c1].bitcast(FP8X4), w1_s[b][a][:, c0:c1], grouped)

        def weave_plain(raw, name):
            grouped = new([P, PACK * 2 * P], BF16, name)
            dst = grouped[:].rearrange("p (c i j) -> p c j i", i=4, j=PACK)
            src = raw[:].rearrange("p j (c i) -> p c j i", i=4)
            return grouped, dst, src

        def w1_first(a):
            grouped, dst, src = weave_plain(w1_head[a], f"w1_bf_head{a}")
            nc.vector.tensor_copy(dst[:, : P // 4], src[:, : P // 4])
            nc.scalar.copy(dst[:, P // 4 :], src[:, P // 4 :])
            quantise_w1(a, 0, 0, P, grouped[:, :PASS])
            quantise_w1(a, 0, P, 2 * P, grouped[:, PASS:])

        def w1_second(a):
            grouped, dst, src = weave_plain(w1_next[a], f"w1_bf_next{a}")
            nc.scalar.copy(dst, src)
            quantise_w1(a, 0, 2 * P, PASS, grouped[:])

        def w1_dealt(a):
            grouped = new([P, PACK * PASS], BF16, f"w1_bf_last{a}")
            nc.scalar.copy(
                grouped[:].rearrange("p (u v m j) -> p u m j v", u=2, v=2, j=PACK),
                w1_last[a][:].rearrange("p j (m u v) -> p u m j v", u=2, v=2),
            )
            quantise_w1(a, 1, 0, PASS, grouped[:])

        def product_w4(b, t, held):
            acc = ps.tile([P, BANK], F32, name=f"acc4_{b}{t}", tag=f"bank{2 + t % 2}")
            for a in range(2):
                nc.tensor.matmul_mx(
                    acc[:],
                    lhsT=w4_w[b][:, a, 2 * P * t : 2 * P * (t + 1)].bitcast(FP4X4),
                    lhsT_scale=w4_s[b][:, a, P * t : P * (t + 1)],
                    rhs=v_w[a][:].bitcast(FP8X4), rhs_scale=v_s[a][:],
                    start=(a == 0), stop=(a == 1),
                )
            nc.scalar.copy(held, acc[:])
            return held

        def refresh(b, t, h=None):
            sum4 = sums4[b, t]
            acc = ps.tile([P, BANK], F32, name=f"acc1_{b}{t}", tag=f"bank{4 + t}")
            for a in range(2):
                nc.tensor.matmul_mx(
                    acc[:],
                    lhsT=w1_w[b][a][:, P * t : P * (t + 1)].bitcast(FP8X4),
                    lhsT_scale=w1_s[b][a][:, P * t : P * (t + 1)],
                    rhs=v_w[a][:].bitcast(FP8X4), rhs_scale=v_s[a][:],
                    start=(a == 0), stop=(a == 1),
                )
            if h is None:
                h = new([P, S], F32, f"h{b}{t}", tag="h", bufs=2)[:]
            nc.vector.tensor_tensor(h, acc[:], sum4, ALU.max)
            nc.vector.tensor_tensor(pages[b, t][:].indirect(idx3[:]), h, wgs_t[t][:] if b else wgs_plain[:], ALU.mult)

        def quantise_x(b, half, grouped, codes, scales):
            nc.vector.quantize_mx(
                codes[:, half * BANK : (half + 1) * BANK].bitcast(FP8X4),
                scales[:, half * BANK : (half + 1) * BANK],
                grouped[:, half * BANK : (half + 1) * BANK, :].rearrange("p n t -> p (n t)"),
            )

        w1_first(0)
        w1_first(1)
        sums4 = {(0, 0): product_w4(0, 0, new([P, S], F32, "sum4_first", tag="w1raw0_0")[:])}
        refresh(0, 0)
        sums4[0, 1] = product_w4(0, 1, new([P, S], F32, "sum4_second", tag="w1raw1_0")[:])
        refresh(0, 1)
        w1_second(0)
        w1_second(1)
        sum4_third = new([P, 2, S], F32, "sum4_third", tag="w1raw1_256")
        for t in (2, 3):
            sums4[0, t] = product_w4(0, t, sum4_third[:, t - 2, :])
        refresh(0, 2)
        w1_dealt(0)
        w1_dealt(1)
        sum4_last = new([P, PACK, S], F32, "sum4_last")
        for t in range(2):
            sums4[1, t] = product_w4(1, t, sum4_last[:, t, :])
        refresh(0, 3, new([P, S], F32, "h03", tag="w1_bf_last1")[:])

        h_pair = new([P, 2, S], F32, "h_pair", tag="w1_bf_last1")
        refresh(1, 0, h_pair[:, 0, :])
        refresh(1, 1, h_pair[:, 1, :])

        row_pairs = new([P, T2 // P, 2, P], F32, "row_pairs", tag="w1raw0_512")
        late = new([P, PACK - 1, T2], BF16, "x_plane_late", tag="w1raw1_512")
        planes = [new([P, T2], BF16, "x_plane0")[:]] + [late[:, c, :] for c in range(PACK - 1)]
        for c in range(PACK):
            nc.scalar.activation(planes[c], pages[0, c][:], ACT.Copy, scale=gains0[:, c : c + 1])
            turned = ps.tile([P, T2 // P, P], BF16, name=f"turned{c}", tag=f"bank{c % 2}")
            for k in range(T2 // P):
                nc.tensor.transpose(turned[:, k, :], planes[c][:, k * P : (k + 1) * P], ident_bf[:])
            nc.scalar.copy(
                row_pairs[:, :, :, 32 * c : 32 * (c + 1)], turned[:].bitcast(F32).rearrange("p k (w u) -> p k u w", u=2)
            )
        x_bf0 = new([P, T2, PACK], BF16, "x_bf0")
        x_pairs = x_bf0[:].bitcast(F32)
        for g in range(T2 // (2 * P)):
            back = ps.tile([P, 2, 2, P], F32, name=f"back{g}", tag=f"bank{g % 2}")
            for k in range(2):
                for u in range(2):
                    nc.tensor.transpose(back[:, k, u, :], row_pairs[:, 2 * g + k, u, :], ident_words[:])
            nc.scalar.copy(
                x_pairs[:, 2 * P * g : 2 * P * (g + 1), :].rearrange("p (k n) u -> p k n u", k=2),
                back[:].rearrange("p k u n -> p k n u"),
            )
        x_s = [new([P, T2], U8, "x_s0", tag="tab2_sc"), new([P, T2], U8, "x_s1")]

        x_w = [new([P, T2], U32, "x_w0", tag="w1_bf_last1"), new([P, T2], U32, "x_w1")]

        for t in (2, 3):
            sums4[1, t] = product_w4(1, t, sum4_last[:, t, :])

        def gather_candidates(first, count, words_tag):
            lst = idx2[:, first // 16 : (first + count) // 16]
            words = new([P, 2, count], U32, f"v2_w{first}", tag=words_tag)
            for a in range(2):
                nc.vector.tensor_copy(words[:, a, :], tab2_w[a][:].bitcast(U32).indirect(lst))
            return words

        v2_first = gather_candidates(0, P, None)
        v2_s = new([P, S2], U8, "v2_s")
        nc.vector.tensor_copy(v2_s[:], tab2_sc[:].indirect(idx2[:]))
        for half in range(2):
            quantise_x(0, half, x_bf0, x_w[0], x_s[0])

        x_bf1 = new([P, T2, PACK], BF16, "x_bf1", tag="w1raw0_512")
        for t in range(2):
            nc.scalar.activation(x_bf1[:, :, t], pages[1, t][:], ACT.Copy, scale=gains1[:, t : t + 1])
        h_last = new([P, 2, S], F32, "h_last", tag="x_bf0")
        refresh(1, 2, h_last[:, 0, :])
        gain_now = new([P, 1], F32, "gain_now")
        nc.scalar.copy(gain_now[:], gains1[:, 2:3])
        nc.scalar.activation(x_bf1[:, :WEAVE_VECTOR, 2], pages[1, 2][:, :WEAVE_VECTOR], ACT.Copy, scale=gain_now[:])
        gain_last = new([P, 2], F32, "gain_last", tag="gain_now")
        nc.scalar.copy(gain_last[:], gains1[:, 2:4])
        nc.scalar.activation(x_bf1[:, WEAVE_VECTOR:, 2], pages[1, 2][:, WEAVE_VECTOR:], ACT.Copy, scale=gain_last[:, 0:1])
        refresh(1, 3, h_last[:, 1, :])
        nc.vector.tensor_scalar(x_bf1[:, :WEAVE_VECTOR, 3], pages[1, 3][:, :WEAVE_VECTOR], gain_last[:, 1:2], None, ALU.mult)
        nc.scalar.activation(x_bf1[:, WEAVE_VECTOR:, 3], pages[1, 3][:, WEAVE_VECTOR:], ACT.Copy, scale=gains1[:, 3:4])
        for half in range(2):
            quantise_x(1, half, x_bf1, x_w[1], x_s[1])
        v2_rest = gather_candidates(P, S2 - P, "w1raw0_512")

        scores = []
        for m in range(S2 // P):
            rows = slice(m * P, (m + 1) * P)
            e = new([P, T2], F32, f"e{m}", tag=f"page0{m}")
            v2_w = v2_first if m == 0 else v2_rest[:, :, (m - 1) * P : m * P]
            scores.append(e)
            for half in range(2):
                cols = slice(half * BANK, (half + 1) * BANK)
                acc = ps.tile([P, BANK], F32, name=f"acc_e{m}{half}", tag=f"bank{2 * m + half}")
                for b in range(2):
                    nc.tensor.matmul_mx(
                        acc[:],
                        lhsT=v2_w[:, b, :].bitcast(FP8X4), lhsT_scale=v2_s[4 * b :, rows],
                        rhs=x_w[b][:, cols].bitcast(FP8X4), rhs_scale=x_s[b][:, cols],
                        start=(b == 0), stop=(b == 1),
                    )
                nc.scalar.copy(e[:, cols], acc[:])

        for m, e in enumerate(scores):
            rows = slice(m * P, (m + 1) * P)
            floor = new([P, PAIRS], F32, f"floor{m}")
            diff = new([P, PAIRS], F32, f"diff{m}")
            res = new([P, PAIRS], F32, f"res{m}")
            last = m == len(scores) - 1
            cuts = (0, LAST_SCALAR if last else PAIRS // 2, PAIRS)
            for c0, c1 in zip(cuts, cuts[1:]):
                nc.vector.tensor_copy(floor[:, c0:c1], e[:].indirect(p2[:, c0 // 16 : c1 // 16]))
            for c0, c1 in zip(cuts, cuts[1:]):
                nc.vector.tensor_tensor(
                    diff[:, c0:c1], e[:].indirect(p1[:, c0 // 16 : c1 // 16]), floor[:, c0:c1], ALU.subtract
                )
            width = LAST_SCALAR if last else PAIRS
            size = new([P, width], F32, f"size{m}", tag="size")
            nc.scalar.activation(size[:], diff[:, :width], ACT.Abs)
            nc.scalar.activation(res[:, :width], size[:], ACT.Identity, bias=seams[:, m : m + 1])
            if last:
                size_end = new([P, PAIRS - width], F32, "size_end")
                nc.vector.scalar_tensor_tensor(size_end[:], diff[:, width:], -1.0, diff[:, width:], ALU.mult, ALU.max)
                nc.vector.tensor_scalar(res[:, width:], size_end[:], seams[:, m : m + 1], None, ALU.add)
            nc.sync.dma_start(out[rows, :], res[:])
